import numpy as np
import ml_dtypes


def mxq(x, axis, fmt="e4m3"):
    dtype, down = {"e4m3": (ml_dtypes.float8_e4m3fn, 7), "e5m2": (ml_dtypes.float8_e5m2, 14)}[fmt]
    v = np.moveaxis(np.asarray(x, np.float32).astype(ml_dtypes.bfloat16).astype(np.float64), axis, -1)
    blocks = v.reshape(v.shape[:-1] + (-1, 32))
    amax = np.abs(blocks).max(-1, keepdims=True)
    byte = np.maximum(np.where(amax > 0, np.frexp(amax)[1] - 1 + 127, 0) - down, 1)
    scale = np.exp2(byte - 127.0)
    codes = (blocks / scale).astype(np.float32).astype(dtype).astype(np.float64)
    return np.moveaxis((codes * scale).reshape(v.shape), -1, axis)


WIDE = False


def mx_kscale(k):
    if not WIDE:
        return np.ones(k)
    levels = np.array([10, -10, 5, -5, 0])
    if k % 512:
        return np.exp2(np.random.permutation(np.resize(levels, k // 32))).repeat(32)
    a = np.empty((k // 512, 16))
    for p in range(k // 512):
        a[p, :8] = np.random.permutation(np.resize(levels, 8))
        for g in range(8):
            far = levels[np.abs(levels - a[p, g]) >= 10]
            a[p, g + 8] = far[np.random.randint(len(far))]
    return np.exp2(a.ravel()).repeat(32)


BF16 = ml_dtypes.bfloat16


def bf(x):
    return np.asarray(x, np.float32).astype(BF16)


def f64(x):
    return np.asarray(x).astype(np.float64)


E2M1 = np.array([0.0, 0.5, 1.0, 1.5, 2.0, 3.0, 4.0, 6.0, -0.0, -0.5, -1.0, -1.5, -2.0, -3.0, -4.0, -6.0])


def pack_weight(w, fmt):
    k, n = w.shape
    w = f64(bf(w)).reshape(k // 32, 32, n)
    amax = np.abs(w).max(1)
    if fmt == "e4m3":
        byte = np.frexp(amax)[1] - 1 + 127 - 7
    else:
        mant, ex = np.frexp(amax / 6.0)
        byte = np.where(mant > 0.5, ex, ex - 1) + 127
    byte = np.clip(np.where(amax > 0, byte, 1), 1, 254)
    scaled = (w * np.exp2(127.0 - byte)[:, None, :]).reshape(k, n).astype(np.float32)
    by_word = np.ascontiguousarray(scaled.reshape(k // 512, 128, 4, n).transpose(0, 1, 3, 2))
    if fmt == "e4m3":
        words = by_word.astype(ml_dtypes.float8_e4m3fn).view(np.uint8)
    else:
        c = by_word.astype(ml_dtypes.float4_e2m1fn).view(np.uint8) & 0xF
        words = c[..., 0::2] | (c[..., 1::2] << 4)
    return np.ascontiguousarray(words), np.ascontiguousarray(byte.astype(np.uint8).reshape(k // 512, 16, n))


def unpack_weight(words, scales, fmt):
    g, p, n, _ = words.shape
    if fmt == "e4m3":
        vals = np.ascontiguousarray(words).view(ml_dtypes.float8_e4m3fn).astype(np.float64)
    else:
        nib = np.empty((g, p, n, 4), np.uint8)
        nib[..., 0::2] = words & 0xF
        nib[..., 1::2] = words >> 4
        vals = E2M1[nib]
    vals = vals * np.repeat(np.exp2(scales.astype(np.float64) - 127.0), 8, axis=1)[..., None]
    return vals.transpose(0, 1, 3, 2).reshape(g * 512, n)
def pack4(w):
    words, scales = pack_weight(w, "e2m1")
    return words.reshape(words.shape[0], 128, -1), scales


def unpack4(words, scales):
    return unpack_weight(words.reshape(words.shape[0], 128, -1, 2), scales, "e2m1")


T, F1, F2, D = 768, 1536, 3072, 1024
THETA, SPREAD, BIAS = 0.5, 0.1, 0.3


def setup_inputs():
    u, v = mx_kscale(F1), mx_kscale(F2)
    near_pre = np.random.standard_normal((T, F1)) * u
    far_pre = np.random.standard_normal((T, F2)) * v
    near_theta = (THETA + SPREAD * np.abs(np.random.standard_normal(F1))) * u
    far_theta = (THETA + SPREAD * np.abs(np.random.standard_normal(F2))) * v
    near_dec = np.random.standard_normal((F1, D)) / np.sqrt(F1) / u[:, None]
    far_words, far_scales = pack4(np.random.standard_normal((F2, D)) / np.sqrt(F2) / v[:, None])
    return {"near_pre": bf(near_pre),
            "far_pre": bf(far_pre),
            "near_theta": bf(near_theta),
            "far_theta": bf(far_theta),
            "near_dec": bf(near_dec),
            "far_words": far_words,
            "far_scales": far_scales,
            "bias": bf(BIAS * np.random.standard_normal(D))}


def reference(near_pre, far_pre, near_theta, far_theta, near_dec, far_words, far_scales, bias):
    zn, zf = f64(near_pre), f64(far_pre)
    an = zn * (zn > f64(near_theta))
    af = zf * (zf > f64(far_theta))
    near = mxq(an, 1, "e4m3") @ mxq(f64(near_dec), 0, "e4m3")
    far = mxq(af, 1, "e4m3") @ unpack4(far_words, far_scales)
    return near + far + f64(bias)

@@ -1,0 +1,266 @@
+from contextlib import ExitStack
+
+import concourse.mybir as mybir
+from concourse.masks import make_identity
+
+T, F1, F2, D = 768, 1536, 3072, 1024
+FLOPS = 2 * T * (F1 + F2) * D
+
+F32 = mybir.dt.float32
+BF16 = mybir.dt.bfloat16
+I32 = mybir.dt.int32
+U32 = mybir.dt.uint32
+U8 = mybir.dt.uint8
+E4M3 = mybir.dt.float8_e4m3fn_x4
+E2M1 = mybir.dt.float4_e2m1fn_x4
+ALU = mybir.AluOpType
+ACT = mybir.ActivationFunctionType
+STEEP = 2.0**17
+TINY = 2.0**-100
+
+P = 128
+KP = 512
+PAIR = 256
+HALF = 512
+NPAIR = T // PAIR
+NF, NN = F2 // KP, F1 // KP
+
+
+def tile_cross_layer_transcoder_s1_kernel(tc, near_pre, far_pre, near_theta, far_theta, near_dec, far_words, far_scales, bias, out):
+    nc = tc.nc
+    with ExitStack() as ctx:
+        keep = ctx.enter_context(tc.tile_pool(name="keep", bufs=1))
+        work = ctx.enter_context(tc.tile_pool(name="work", bufs=3))
+        psum_t = ctx.enter_context(tc.psum_pool(name="psum_t", bufs=4))
+        psum_a = ctx.enter_context(tc.psum_pool(name="psum_a", bufs=1))
+        ctx.enter_context(tc.manual_schedule())
+
+        ident = keep.tile([P, P], F32, name="ident")
+        make_identity(nc, ident[:])
+
+        planes = keep.tile([P, NF, D], U8, name="planes", align_bytes=64)
+        nc.vector.memset(planes[:].rearrange("p g n -> p (g n)").bitcast(I32), 0)
+
+        th = {}
+        th["f"] = keep.tile([P, NF, 4], BF16, name="th_f")
+        th["n"] = keep.tile([P, NN, 4], BF16, name="th_n")
+        nc.scalar.dma_start(out=th["f"][:], in_=far_theta.rearrange("(g p t) -> p g t", p=P, t=4))
+        nc.scalar.dma_start(out=th["n"][:], in_=near_theta.rearrange("(g p t) -> p g t", p=P, t=4))
+        for q in range(4):
+            nc.scalar.dma_start(
+                out=planes[32 * q : 32 * q + 4, :, :].bitcast(I32),
+                in_=far_scales[:, 4 * q : 4 * q + 4, :].rearrange("g r n -> r g n").bitcast(I32),
+            )
+
+        steep, shift = {}, {}
+
+        def prepare_sigmoid(kind, n):
+            size = th[kind][:].rearrange("p g t -> p (g t)")
+            mag = keep.tile([P, 4 * n], F32, name="mag_" + kind)
+            nc.scalar.activation(out=mag[:], in_=size, func=ACT.Abs)
+            nc.vector.tensor_scalar_max(mag[:], mag[:], TINY)
+            inv = keep.tile([P, 4 * n], F32, name="inv_" + kind)
+            nc.vector.reciprocal(out=inv[:], in_=mag[:])
+            k = keep.tile([P, 4 * n], F32, name="steep_" + kind)
+            nc.gpsimd.tensor_scalar(out=k[:], in0=inv[:], scalar1=STEEP, scalar2=0.0, op0=ALU.mult, op1=ALU.add)
+            b = keep.tile([P, 4 * n], F32, name="shift_" + kind)
+            nc.gpsimd.tensor_tensor(out=b[:], in0=k[:], in1=size, op=ALU.mult)
+            nc.gpsimd.tensor_scalar(out=b[:], in0=b[:], scalar1=-1.0, scalar2=-STEEP / 512, op0=ALU.mult, op1=ALU.add)
+            steep[kind], shift[kind] = k, b
+
+        x = {}
+
+        def load_x(kind, pair, g0, n):
+            src = far_pre if kind == "f" else near_pre
+            t = keep.tile([P, 2, n * KP], BF16, name="x_%s%d_%d" % (kind, pair, g0))
+            nc.sync.dma_start(
+                out=t[:],
+                in_=src[pair * PAIR : (pair + 1) * PAIR, g0 * KP : (g0 + n) * KP].rearrange("(a p) k -> p a k", p=P),
+            )
+            for i in range(n):
+                x[kind, pair, g0 + i] = t[:].rearrange("p a k -> p (a k)").bitcast(F32), n * KP // 2, i * KP // 2
+
+        words = {}
+
+        def load_words(g0):
+            t = keep.tile([P, 2, 2 * D], U8, name="words_%d" % g0, align_bytes=64)
+            nc.sync.dma_start(out=t[:].bitcast(I32), in_=far_words[g0 : g0 + 2].rearrange("g p n -> p g n").bitcast(I32))
+            words[g0] = t[:, 0, :]
+            words[g0 + 1] = t[:, 1, :]
+
+        draw = {}
+
+        def load_dec(g):
+            t = keep.tile([P, 4, D], BF16, name="draw_%d" % g)
+            nc.sync.dma_start(out=t[:], in_=near_dec[g * KP : (g + 1) * KP].rearrange("(p j) n -> p j n", j=4))
+            draw[g] = t
+
+        load_x("f", 0, 0, 2)
+        load_words(0)
+        load_x("f", 0, 2, 2)
+        load_words(2)
+        load_dec(0)
+        load_x("f", 0, 4, 2)
+        load_words(4)
+        load_x("n", 0, 0, 3)
+        load_dec(1)
+        load_dec(2)
+        bias_bc = keep.tile([P, D], BF16, name="bias_bc")
+        nc.sync.dma_start(out=bias_bc[:], in_=bias.partition_broadcast(P))
+        for pair in range(1, NPAIR):
+            for g0 in range(0, NF, 2):
+                load_x("f", pair, g0, 2)
+            load_x("n", pair, 0, 3)
+
+        dint, dcode, dscale = {}, {}, {}
+
+        def dec_interleave(g, c):
+            if c == 0:
+                dint[g] = keep.tile([P, 4 * D], BF16, name="dint_%d" % g, align_bytes=64)
+            cols = slice(c * 256, (c + 1) * 256)
+            nc.scalar.copy(
+                out=dint[g][:, c * 1024 : (c + 1) * 1024].rearrange("p (n j) -> p n j", j=4),
+                in_=draw[g][:, :, cols].rearrange("p j n -> p n j"),
+            )
+
+        def dec_quantize(g):
+            code = keep.tile([P, D], U32, name="dcode_%d" % g, align_bytes=64)
+            scale = keep.tile([P, D], U8, name="dscale_%d" % g, align_bytes=64)
+            for h in range(2):
+                cols = slice(h * HALF, (h + 1) * HALF)
+                nc.vector.quantize_mx(out=code[:, cols].bitcast(E4M3), scales=scale[:, cols], in_=dint[g][:, h * 2048 : (h + 1) * 2048])
+            dcode[g], dscale[g] = code, scale
+
+
+        steps = [(pair, kind, g) for pair in range(NPAIR) for kind, n in (("f", NF), ("n", NN)) for g in range(n)]
+        n_steps = len(steps)
+        bank, mask, an, code, scale = {}, {}, {}, {}, {}
+
+        def transposes(s):
+            pair, kind, g = steps[s]
+            w, tile_words, off = x[kind, pair, g]
+            b = psum_t.tile([P, 2, PAIR], F32, name="bank")
+            for u in range(2):
+                for a in range(2):
+                    first = a * tile_words + off + u
+                    nc.tensor.transpose(b[:, u, a * P : (a + 1) * P], w[:, first : first + 2 * P - 1 : 2], ident[:])
+            bank[s] = b[:].rearrange("p u r -> p (u r)").bitcast(BF16).rearrange("p (u r e) -> p r u e", u=2, e=2)
+
+        def scalar_mask(s):
+            kind, g = steps[s][1:]
+            m = work.tile([P, 4 * PAIR], BF16, name="mask_s", bufs=4)
+            view = m[:].rearrange("p (u r e) -> p r u e", u=2, e=2)
+            for u in range(2):
+                for e in range(2):
+                    j = 4 * g + 2 * u + e
+                    nc.scalar.activation(
+                        out=view[:, :, u, e],
+                        in_=bank[s][:, :, u, e],
+                        func=ACT.Sigmoid,
+                        bias=shift[kind][:, j : j + 1],
+                        scale=steep[kind][:, j : j + 1],
+                    )
+            mask[s] = view
+
+        def make_mask(s):
+            kind, g = steps[s][1:]
+            m = work.tile([P, 4 * PAIR], BF16, name="mask")
+            view = m[:].rearrange("p (r u e) -> p r u e", u=2, e=2)
+            nc.vector.tensor_tensor(
+                out=view,
+                in0=bank[s],
+                in1=th[kind][:, g : g + 1, :].rearrange("p o (u e) -> p o u e", u=2).to_broadcast([P, PAIR, 2, 2]),
+                op=ALU.is_gt,
+            )
+            mask[s] = view
+
+        def apply_mask(s):
+            t = work.tile([P, 4 * PAIR], BF16, name="an", align_bytes=64)
+            nc.vector.tensor_tensor(
+                out=t[:].rearrange("p (r u e) -> p r u e", u=2, e=2),
+                in0=bank[s],
+                in1=mask[s],
+                op=ALU.mult,
+            )
+            an[s] = t
+
+        def quantize(s):
+            c = keep.tile([P, PAIR], U32, name="code_%d" % s, align_bytes=64)
+            sc = keep.tile([P, PAIR], U8, name="scale_%d" % s, align_bytes=64)
+            nc.vector.quantize_mx(out=c[:].bitcast(E4M3), scales=sc[:], in_=an[s][:])
+            code[s], scale[s] = c, sc
+
+        acc = {}
+
+        def multiply(group):
+            for a in range(2):
+                for h in range(2):
+                    for s in group:
+                        pair, kind, g = steps[s]
+                        first = kind == "f" and g == 0
+                        if first:
+                            acc[pair, a, h] = psum_a.tile([P, HALF], F32, name="acc_%d%d" % (a, h))
+                        if kind == "f":
+                            rhs = words[g][:, h * 2 * HALF : (h + 1) * 2 * HALF].bitcast(E2M1)
+                            rhs_scale = planes[:, g, h * HALF : (h + 1) * HALF]
+                        else:
+                            rhs = dcode[g][:, h * HALF : (h + 1) * HALF].bitcast(E4M3)
+                            rhs_scale = dscale[g][:, h * HALF : (h + 1) * HALF]
+                        nc.tensor.matmul_mx(
+                            out=acc[pair, a, h][:],
+                            lhsT=code[s][:, a * P : (a + 1) * P].bitcast(E4M3),
+                            lhsT_scale=scale[s][:, a * P : (a + 1) * P],
+                            rhs=rhs,
+                            rhs_scale=rhs_scale,
+                            start=first,
+                            stop=(kind == "n" and g == NN - 1),
+                        )
+
+        def finish(pair):
+            for a in range(2):
+                res = work.tile([P, D], F32, name="res")
+                for h in range(2):
+                    cols = slice(h * HALF, (h + 1) * HALF)
+                    nc.vector.tensor_tensor(out=res[:, cols], in0=acc[pair, a, h][:], in1=bias_bc[:, cols], op=ALU.add)
+                row = pair * PAIR + a * P
+                nc.sync.dma_start(out=out[row : row + P, :], in_=res[:])
+
+        groups = [[0], [1, 2], [3, 4], [5, 6], [7, 8], [9, 10], [11, 12], [13, 14], [15, 16], [17],
+                  [18, 19], [20, 21], [22, 23], [24, 25], [26]]
+        group_at = {g[-1] + 2: g for g in groups}
+        finish_at = {11: 0, 20: 1, 28: 2}
+        dec_at = {6: 0, 7: 1, 8: 2}
+
+        on_scalar = {1, 3} | {s for s in range(9, n_steps) if s % 3}
+
+        def transpose_and_mask(s):
+            transposes(s)
+            if s in on_scalar:
+                scalar_mask(s)
+
+        prepare_sigmoid("f", NF)
+        prepare_sigmoid("n", NN)
+        transpose_and_mask(0)
+        transpose_and_mask(1)
+        make_mask(0)
+        dec_pieces = [(g, c) for g in range(NN) for c in range(4)]
+        for i in range(n_steps + 2):
+            if i % 2 == 0:
+                for s in (i + 2, i + 3):
+                    if s < n_steps:
+                        transpose_and_mask(s)
+            if i < 6:
+                for g, c in dec_pieces[2 * i : 2 * i + 2]:
+                    dec_interleave(g, c)
+            if i in group_at:
+                multiply(group_at[i])
+            if i + 1 < n_steps and i + 1 not in on_scalar:
+                make_mask(i + 1)
+            if i in dec_at:
+                dec_quantize(dec_at[i])
+            if i < n_steps:
+                apply_mask(i)
+            if i in finish_at:
+                finish(finish_at[i])
+            if 0 <= i - 1 < n_steps:
+                quantize(i - 1)

@@ -47,7 +47,7 @@ def tile_cross_layer_transcoder_s1_kernel(tc, near_pre, far_pre, near_theta, far
         nc.scalar.dma_start(out=th["f"][:], in_=far_theta.rearrange("(g p t) -> p g t", p=P, t=4))
         nc.scalar.dma_start(out=th["n"][:], in_=near_theta.rearrange("(g p t) -> p g t", p=P, t=4))
         for q in range(4):
-            nc.scalar.dma_start(
+            nc.gpsimd.dma_start(
                 out=planes[32 * q : 32 * q + 4, :, :].bitcast(I32),
                 in_=far_scales[:, 4 * q : 4 * q + 4, :].rearrange("g r n -> r g n").bitcast(I32),
             )
@@ -95,22 +95,28 @@ def tile_cross_layer_transcoder_s1_kernel(tc, near_pre, far_pre, near_theta, far
             nc.sync.dma_start(out=t[:], in_=near_dec[g * KP : (g + 1) * KP].rearrange("(p j) n -> p j n", j=4))
             draw[g] = t
 
-        load_x("f", 0, 0, 2)
+        load_x("f", 0, 0, 1)
+        load_x("f", 0, 1, 1)
         load_words(0)
         load_x("f", 0, 2, 2)
         load_words(2)
         load_dec(0)
-        load_x("f", 0, 4, 2)
-        load_words(4)
-        load_x("n", 0, 0, 3)
+        load_x("n", 0, 0, 1)
         load_dec(1)
+        load_x("n", 0, 1, 1)
         load_dec(2)
+        load_x("f", 0, 4, 2)
+        load_x("n", 0, 2, 1)
+        load_words(4)
+        load_x("f", 1, 0, 2)
         bias_bc = keep.tile([P, D], BF16, name="bias_bc")
         nc.sync.dma_start(out=bias_bc[:], in_=bias.partition_broadcast(P))
-        for pair in range(1, NPAIR):
-            for g0 in range(0, NF, 2):
-                load_x("f", pair, g0, 2)
-            load_x("n", pair, 0, 3)
+        load_x("f", 1, 2, 2)
+        load_x("f", 1, 4, 2)
+        load_x("n", 1, 0, 3)
+        for g0 in range(0, NF, 2):
+            load_x("f", 2, g0, 2)
+        load_x("n", 2, 0, 3)
 
         dint, dcode, dscale = {}, {}, {}
 
@@ -118,23 +124,37 @@ def tile_cross_layer_transcoder_s1_kernel(tc, near_pre, far_pre, near_theta, far
             if c == 0:
                 dint[g] = keep.tile([P, 4 * D], BF16, name="dint_%d" % g, align_bytes=64)
             cols = slice(c * 256, (c + 1) * 256)
-            nc.scalar.copy(
-                out=dint[g][:, c * 1024 : (c + 1) * 1024].rearrange("p (n j) -> p n j", j=4),
-                in_=draw[g][:, :, cols].rearrange("p j n -> p n j"),
-            )
+            new = dint[g][:, c * 1024 : (c + 1) * 1024].rearrange("p (n j) -> p n j", j=4)
+            old = draw[g][:, :, cols].rearrange("p j n -> p n j")
+            if c % 2 == 0:
+                nc.scalar.copy(out=new, in_=old)
+            else:
+                nc.gpsimd.tensor_scalar(out=new, in0=old, scalar1=1.0, scalar2=0.0, op0=ALU.mult, op1=ALU.add)
 
-        def dec_quantize(g):
-            code = keep.tile([P, D], U32, name="dcode_%d" % g, align_bytes=64)
-            scale = keep.tile([P, D], U8, name="dscale_%d" % g, align_bytes=64)
-            for h in range(2):
-                cols = slice(h * HALF, (h + 1) * HALF)
-                nc.vector.quantize_mx(out=code[:, cols].bitcast(E4M3), scales=scale[:, cols], in_=dint[g][:, h * 2048 : (h + 1) * 2048])
-            dcode[g], dscale[g] = code, scale
+        def dec_quantize(g, h):
+            if h == 0:
+                dcode[g] = keep.tile([P, D], U32, name="dcode_%d" % g, align_bytes=64)
+                dscale[g] = keep.tile([P, D], U8, name="dscale_%d" % g, align_bytes=64)
+            cols = slice(h * HALF, (h + 1) * HALF)
+            nc.vector.quantize_mx(out=dcode[g][:, cols].bitcast(E4M3), scales=dscale[g][:, cols], in_=dint[g][:, h * 2048 : (h + 1) * 2048])
 
 
-        steps = [(pair, kind, g) for pair in range(NPAIR) for kind, n in (("f", NF), ("n", NN)) for g in range(n)]
+        mixed = [("f", 0), ("f", 1), ("f", 2), ("f", 3), ("n", 0), ("n", 1), ("f", 4), ("n", 2), ("f", 5)]
+        steps = [(pair, kind, g) for pair in range(NPAIR) for kind, g in mixed]
         n_steps = len(steps)
         bank, mask, an, code, scale = {}, {}, {}, {}, {}
+
+        split = {}
+
+        def permute(s):
+            pair, kind, g = steps[s]
+            w, tile_words, off = x[kind, pair, g]
+            t = work.tile([P, 2, 2, P], F32, name="split", bufs=5)
+            nc.scalar.copy(
+                out=t[:],
+                in_=w.rearrange("p (a k) -> p a k", a=2)[:, :, off : off + 2 * P].rearrange("p a (w u) -> p a u w", u=2),
+            )
+            split[s] = t
 
         def transposes(s):
             pair, kind, g = steps[s]
@@ -143,7 +163,8 @@ def tile_cross_layer_transcoder_s1_kernel(tc, near_pre, far_pre, near_theta, far
             for u in range(2):
                 for a in range(2):
                     first = a * tile_words + off + u
-                    nc.tensor.transpose(b[:, u, a * P : (a + 1) * P], w[:, first : first + 2 * P - 1 : 2], ident[:])
+                    some = split[s][:, a, u, :] if s in split else w[:, first : first + 2 * P - 1 : 2]
+                    nc.tensor.transpose(b[:, u, a * P : (a + 1) * P], some, ident[:])
             bank[s] = b[:].rearrange("p u r -> p (u r)").bitcast(BF16).rearrange("p (u r e) -> p r u e", u=2, e=2)
 
         def scalar_mask(s):
@@ -213,54 +234,55 @@ def tile_cross_layer_transcoder_s1_kernel(tc, near_pre, far_pre, near_theta, far
                             rhs=rhs,
                             rhs_scale=rhs_scale,
                             start=first,
-                            stop=(kind == "n" and g == NN - 1),
+                            stop=(kind == "f" and g == NF - 1),
                         )
 
         def finish(pair):
             for a in range(2):
-                res = work.tile([P, D], F32, name="res")
+                row = pair * PAIR + a * P
                 for h in range(2):
                     cols = slice(h * HALF, (h + 1) * HALF)
-                    nc.vector.tensor_tensor(out=res[:, cols], in0=acc[pair, a, h][:], in1=bias_bc[:, cols], op=ALU.add)
-                row = pair * PAIR + a * P
-                nc.sync.dma_start(out=out[row : row + P, :], in_=res[:])
+                    res = work.tile([P, HALF], F32, name="res", bufs=4)
+                    nc.vector.tensor_tensor(out=res[:], in0=acc[pair, a, h][:], in1=bias_bc[:, cols], op=ALU.add)
+                    nc.sync.dma_start(out=out[row : row + P, cols], in_=res[:])
 
-        groups = [[0], [1, 2], [3, 4], [5, 6], [7, 8], [9, 10], [11, 12], [13, 14], [15, 16], [17],
-                  [18, 19], [20, 21], [22, 23], [24, 25], [26]]
-        group_at = {g[-1] + 2: g for g in groups}
-        finish_at = {11: 0, 20: 1, 28: 2}
-        dec_at = {6: 0, 7: 1, 8: 2}
-
-        on_scalar = {1, 3} | {s for s in range(9, n_steps) if s % 3}
-
-        def transpose_and_mask(s):
-            transposes(s)
-            if s in on_scalar:
-                scalar_mask(s)
+        waves = [[0], [1], [2, 3], [4], [5], [6, 7], [8], [9, 10], [11, 12], [13, 14], [15, 16], [17, 18], [19, 20], [21, 22], [23, 24], [25, 26]]
+        products = [[0], [1], [2, 3], [4], [5], [6, 7], [8], [9, 10], [11, 12], [13, 14], [15, 16], [17], [18, 19, 20], [21, 22], [23, 24], [25, 26]]
+        dec_after = {3: [(0, 0), (0, 1)], 4: [(1, 0), (1, 1)], 5: [(2, 0), (2, 1)]}
+        on_scalar = {w[-1] for w in waves if w[0] > 9 and len(w) == 2}
+        permuted = {s for s in range(9, n_steps)}
 
         prepare_sigmoid("f", NF)
         prepare_sigmoid("n", NN)
-        transpose_and_mask(0)
-        transpose_and_mask(1)
-        make_mask(0)
-        dec_pieces = [(g, c) for g in range(NN) for c in range(4)]
-        for i in range(n_steps + 2):
-            if i % 2 == 0:
-                for s in (i + 2, i + 3):
-                    if s < n_steps:
-                        transpose_and_mask(s)
-            if i < 6:
-                for g, c in dec_pieces[2 * i : 2 * i + 2]:
-                    dec_interleave(g, c)
-            if i in group_at:
-                multiply(group_at[i])
-            if i + 1 < n_steps and i + 1 not in on_scalar:
-                make_mask(i + 1)
-            if i in dec_at:
-                dec_quantize(dec_at[i])
-            if i < n_steps:
-                apply_mask(i)
-            if i in finish_at:
-                finish(finish_at[i])
-            if 0 <= i - 1 < n_steps:
-                quantize(i - 1)
+        for g in range(NN):
+            for c in range(4):
+                dec_interleave(g, c)
+
+        def prepare(w):
+            if w < len(waves):
+                for s in waves[w]:
+                    transposes(s)
+                    if s in on_scalar:
+                        scalar_mask(s)
+
+        prepare(0)
+        for w in range(len(waves) + 1):
+            if w + 2 < len(waves):
+                for s in waves[w + 2]:
+                    if s in permuted:
+                        permute(s)
+            prepare(w + 1)
+            done = products[w - 1] if w > 0 else []
+            multiply(done)
+            now = waves[w] if w < len(waves) else []
+            for s in now:
+                if s not in on_scalar:
+                    make_mask(s)
+            for s in now:
+                apply_mask(s)
+            if done and steps[done[-1]][1:] == mixed[-1]:
+                finish(steps[done[-1]][0])
+            for s in now:
+                quantize(s)
+            for g, h in dec_after.get(w, []):
+                dec_quantize(g, h)

@@ -35,19 +35,18 @@ def tile_cross_layer_transcoder_s1_kernel(tc, near_pre, far_pre, near_theta, far
         psum_a = ctx.enter_context(tc.psum_pool(name="psum_a", bufs=1))
         ctx.enter_context(tc.manual_schedule())
 
-        ident = keep.tile([P, P], F32, name="ident")
-        make_identity(nc, ident[:])
-
         planes = keep.tile([P, NF, D], U8, name="planes", align_bytes=64)
         nc.vector.memset(planes[:].rearrange("p g n -> p (g n)").bitcast(I32), 0)
 
         th = {}
         th["f"] = keep.tile([P, NF, 4], BF16, name="th_f")
         th["n"] = keep.tile([P, NN, 4], BF16, name="th_n")
-        nc.scalar.dma_start(out=th["f"][:], in_=far_theta.rearrange("(g p t) -> p g t", p=P, t=4))
-        nc.scalar.dma_start(out=th["n"][:], in_=near_theta.rearrange("(g p t) -> p g t", p=P, t=4))
+        nc.gpsimd.dma_start(out=th["f"][:], in_=far_theta.rearrange("(g p t) -> p g t", p=P, t=4))
+        ident = keep.tile([P, P], F32, name="ident")
+        make_identity(nc, ident[:])
+        nc.gpsimd.dma_start(out=th["n"][:], in_=near_theta.rearrange("(g p t) -> p g t", p=P, t=4))
         for q in range(4):
-            nc.gpsimd.dma_start(
+            nc.scalar.dma_start(
                 out=planes[32 * q : 32 * q + 4, :, :].bitcast(I32),
                 in_=far_scales[:, 4 * q : 4 * q + 4, :].rearrange("g r n -> r g n").bitcast(I32),
             )
@@ -57,8 +56,8 @@ def tile_cross_layer_transcoder_s1_kernel(tc, near_pre, far_pre, near_theta, far
         def prepare_sigmoid(kind, n):
             size = th[kind][:].rearrange("p g t -> p (g t)")
             mag = keep.tile([P, 4 * n], F32, name="mag_" + kind)
-            nc.scalar.activation(out=mag[:], in_=size, func=ACT.Abs)
-            nc.vector.tensor_scalar_max(mag[:], mag[:], TINY)
+            nc.vector.tensor_scalar(out=mag[:], in0=size, scalar1=-1.0, scalar2=TINY, op0=ALU.mult, op1=ALU.max)
+            nc.vector.tensor_tensor(out=mag[:], in0=mag[:], in1=size, op=ALU.max)
             inv = keep.tile([P, 4 * n], F32, name="inv_" + kind)
             nc.vector.reciprocal(out=inv[:], in_=mag[:])
             k = keep.tile([P, 4 * n], F32, name="steep_" + kind)
@@ -104,10 +103,10 @@ def tile_cross_layer_transcoder_s1_kernel(tc, near_pre, far_pre, near_theta, far
         load_x("n", 0, 0, 1)
         load_dec(1)
         load_x("n", 0, 1, 1)
-        load_dec(2)
         load_x("f", 0, 4, 2)
-        load_x("n", 0, 2, 1)
         load_words(4)
+        load_x("n", 0, 2, 1)
+        load_dec(2)
         load_x("f", 1, 0, 2)
         bias_bc = keep.tile([P, D], BF16, name="bias_bc")
         nc.sync.dma_start(out=bias_bc[:], in_=bias.partition_broadcast(P))
@@ -121,10 +120,10 @@ def tile_cross_layer_transcoder_s1_kernel(tc, near_pre, far_pre, near_theta, far
         dint, dcode, dscale = {}, {}, {}
 
         def dec_interleave(g, c):
-            if c == 0:
+            if g not in dint:
                 dint[g] = keep.tile([P, 4 * D], BF16, name="dint_%d" % g, align_bytes=64)
-            cols = slice(c * 256, (c + 1) * 256)
-            new = dint[g][:, c * 1024 : (c + 1) * 1024].rearrange("p (n j) -> p n j", j=4)
+            cols = slice(c * 128, (c + 1) * 128)
+            new = dint[g][:, c * 512 : (c + 1) * 512].rearrange("p (n j) -> p n j", j=4)
             old = draw[g][:, :, cols].rearrange("p j n -> p n j")
             if c % 2 == 0:
                 nc.scalar.copy(out=new, in_=old)
@@ -139,7 +138,7 @@ def tile_cross_layer_transcoder_s1_kernel(tc, near_pre, far_pre, near_theta, far
             nc.vector.quantize_mx(out=dcode[g][:, cols].bitcast(E4M3), scales=dscale[g][:, cols], in_=dint[g][:, h * 2048 : (h + 1) * 2048])
 
 
-        mixed = [("f", 0), ("f", 1), ("f", 2), ("f", 3), ("n", 0), ("n", 1), ("f", 4), ("n", 2), ("f", 5)]
+        mixed = [("f", 0), ("f", 1), ("f", 2), ("f", 3), ("n", 0), ("n", 1), ("f", 4), ("f", 5), ("n", 2)]
         steps = [(pair, kind, g) for pair in range(NPAIR) for kind, g in mixed]
         n_steps = len(steps)
         bank, mask, an, code, scale = {}, {}, {}, {}, {}
@@ -234,7 +233,7 @@ def tile_cross_layer_transcoder_s1_kernel(tc, near_pre, far_pre, near_theta, far
                             rhs=rhs,
                             rhs_scale=rhs_scale,
                             start=first,
-                            stop=(kind == "f" and g == NF - 1),
+                            stop=(kind == "n" and g == NN - 1),
                         )
 
         def finish(pair):
@@ -246,16 +245,15 @@ def tile_cross_layer_transcoder_s1_kernel(tc, near_pre, far_pre, near_theta, far
                     nc.vector.tensor_tensor(out=res[:], in0=acc[pair, a, h][:], in1=bias_bc[:, cols], op=ALU.add)
                     nc.sync.dma_start(out=out[row : row + P, cols], in_=res[:])
 
-        waves = [[0], [1], [2, 3], [4], [5], [6, 7], [8], [9, 10], [11, 12], [13, 14], [15, 16], [17, 18], [19, 20], [21, 22], [23, 24], [25, 26]]
-        products = [[0], [1], [2, 3], [4], [5], [6, 7], [8], [9, 10], [11, 12], [13, 14], [15, 16], [17], [18, 19, 20], [21, 22], [23, 24], [25, 26]]
-        dec_after = {3: [(0, 0), (0, 1)], 4: [(1, 0), (1, 1)], 5: [(2, 0), (2, 1)]}
-        on_scalar = {w[-1] for w in waves if w[0] > 9 and len(w) == 2}
-        permuted = {s for s in range(9, n_steps)}
+        waves = [[0, 1], [2, 3], [4], [5], [6, 7], [8]] + [[s, s + 1] for s in range(9, n_steps, 2)]
+        products = waves[:9] + [[15, 16], [17], [18, 19, 20], [21, 22], [23, 24], [25, 26]]
+        dec_after = {2: 0, 3: 1, 5: 2}
+        on_scalar = {w[-1] for w in waves if w[0] > 9 and len(w) == 2} | {9, 10}
+        permuted = {s for s in range(13, n_steps)}
 
         prepare_sigmoid("f", NF)
-        prepare_sigmoid("n", NN)
         for g in range(NN):
-            for c in range(4):
+            for c in range(8):
                 dec_interleave(g, c)
 
         def prepare(w):
@@ -271,18 +269,24 @@ def tile_cross_layer_transcoder_s1_kernel(tc, near_pre, far_pre, near_theta, far
                 for s in waves[w + 2]:
                     if s in permuted:
                         permute(s)
-            prepare(w + 1)
+            if w > 3:
+                prepare(w + 1)
             done = products[w - 1] if w > 0 else []
             multiply(done)
+            if w <= 3:
+                prepare(w + 1)
             now = waves[w] if w < len(waves) else []
             for s in now:
                 if s not in on_scalar:
                     make_mask(s)
             for s in now:
                 apply_mask(s)
-            if done and steps[done[-1]][1:] == mixed[-1]:
-                finish(steps[done[-1]][0])
             for s in now:
                 quantize(s)
-            for g, h in dec_after.get(w, []):
-                dec_quantize(g, h)
+            if done and steps[done[-1]][1:] == mixed[-1]:
+                finish(steps[done[-1]][0])
+            if w in dec_after:
+                dec_quantize(dec_after[w], 0)
+                dec_quantize(dec_after[w], 1)
+            if w == 0:
+                prepare_sigmoid("n", NN)

from contextlib import ExitStack

import concourse.mybir as mybir
from concourse.masks import make_identity

T, F1, F2, D = 768, 1536, 3072, 1024
FLOPS = 2 * T * (F1 + F2) * D

F32 = mybir.dt.float32
BF16 = mybir.dt.bfloat16
I32 = mybir.dt.int32
U32 = mybir.dt.uint32
U8 = mybir.dt.uint8
E4M3 = mybir.dt.float8_e4m3fn_x4
E2M1 = mybir.dt.float4_e2m1fn_x4
ALU = mybir.AluOpType
ACT = mybir.ActivationFunctionType
STEEP = 2.0**17
TINY = 2.0**-100

P = 128
KP = 512
PAIR = 256
HALF = 512
NPAIR = T // PAIR
NF, NN = F2 // KP, F1 // KP


def tile_cross_layer_transcoder_s1_kernel(tc, near_pre, far_pre, near_theta, far_theta, near_dec, far_words, far_scales, bias, out):
    nc = tc.nc
    with ExitStack() as ctx:
        keep = ctx.enter_context(tc.tile_pool(name="keep", bufs=1))
        work = ctx.enter_context(tc.tile_pool(name="work", bufs=3))
        psum_t = ctx.enter_context(tc.psum_pool(name="psum_t", bufs=4))
        psum_a = ctx.enter_context(tc.psum_pool(name="psum_a", bufs=1))
        ctx.enter_context(tc.manual_schedule())

        planes = keep.tile([P, NF, D], U8, name="planes", align_bytes=64)
        nc.vector.memset(planes[:].rearrange("p g n -> p (g n)").bitcast(I32), 0)

        th = {}
        th["f"] = keep.tile([P, NF, 4], BF16, name="th_f")
        th["n"] = keep.tile([P, NN, 4], BF16, name="th_n")
        nc.gpsimd.dma_start(out=th["f"][:], in_=far_theta.rearrange("(g p t) -> p g t", p=P, t=4))
        ident = keep.tile([P, P], F32, name="ident")
        make_identity(nc, ident[:])
        nc.gpsimd.dma_start(out=th["n"][:], in_=near_theta.rearrange("(g p t) -> p g t", p=P, t=4))
        for q in range(4):
            nc.scalar.dma_start(
                out=planes[32 * q : 32 * q + 4, :, :].bitcast(I32),
                in_=far_scales[:, 4 * q : 4 * q + 4, :].rearrange("g r n -> r g n").bitcast(I32),
            )

        steep, shift = {}, {}

        def prepare_sigmoid(kind, n):
            size = th[kind][:].rearrange("p g t -> p (g t)")
            mag = keep.tile([P, 4 * n], F32, name="mag_" + kind)
            nc.vector.tensor_scalar(out=mag[:], in0=size, scalar1=-1.0, scalar2=TINY, op0=ALU.mult, op1=ALU.max)
            nc.vector.tensor_tensor(out=mag[:], in0=mag[:], in1=size, op=ALU.max)
            inv = keep.tile([P, 4 * n], F32, name="inv_" + kind)
            nc.vector.reciprocal(out=inv[:], in_=mag[:])
            k = keep.tile([P, 4 * n], F32, name="steep_" + kind)
            nc.gpsimd.tensor_scalar(out=k[:], in0=inv[:], scalar1=STEEP, scalar2=0.0, op0=ALU.mult, op1=ALU.add)
            b = keep.tile([P, 4 * n], F32, name="shift_" + kind)
            nc.gpsimd.tensor_tensor(out=b[:], in0=k[:], in1=size, op=ALU.mult)
            nc.gpsimd.tensor_scalar(out=b[:], in0=b[:], scalar1=-1.0, scalar2=-STEEP / 512, op0=ALU.mult, op1=ALU.add)
            steep[kind], shift[kind] = k, b

        x = {}

        def load_x(kind, pair, g0, n):
            src = far_pre if kind == "f" else near_pre
            t = keep.tile([P, 2, n * KP], BF16, name="x_%s%d_%d" % (kind, pair, g0))
            nc.sync.dma_start(
                out=t[:],
                in_=src[pair * PAIR : (pair + 1) * PAIR, g0 * KP : (g0 + n) * KP].rearrange("(a p) k -> p a k", p=P),
            )
            for i in range(n):
                x[kind, pair, g0 + i] = t[:].rearrange("p a k -> p (a k)").bitcast(F32), n * KP // 2, i * KP // 2

        words = {}

        def load_words(g0):
            t = keep.tile([P, 2, 2 * D], U8, name="words_%d" % g0, align_bytes=64)
            nc.sync.dma_start(out=t[:].bitcast(I32), in_=far_words[g0 : g0 + 2].rearrange("g p n -> p g n").bitcast(I32))
            words[g0] = t[:, 0, :]
            words[g0 + 1] = t[:, 1, :]

        draw = {}

        def load_dec(g):
            t = keep.tile([P, 4, D], BF16, name="draw_%d" % g)
            nc.sync.dma_start(out=t[:], in_=near_dec[g * KP : (g + 1) * KP].rearrange("(p j) n -> p j n", j=4))
            draw[g] = t

        load_x("f", 0, 0, 1)
        load_x("f", 0, 1, 1)
        load_words(0)
        load_x("f", 0, 2, 2)
        load_words(2)
        load_dec(0)
        load_x("n", 0, 0, 1)
        load_dec(1)
        load_x("n", 0, 1, 1)
        load_x("f", 0, 4, 2)
        load_words(4)
        load_x("n", 0, 2, 1)
        load_dec(2)
        load_x("f", 1, 0, 2)
        bias_bc = keep.tile([P, D], BF16, name="bias_bc")
        nc.sync.dma_start(out=bias_bc[:], in_=bias.partition_broadcast(P))
        load_x("f", 1, 2, 2)
        load_x("f", 1, 4, 2)
        load_x("n", 1, 0, 3)
        for g0 in range(0, NF, 2):
            load_x("f", 2, g0, 2)
        load_x("n", 2, 0, 3)

        dint, dcode, dscale = {}, {}, {}

        def dec_interleave(g, c):
            if g not in dint:
                dint[g] = keep.tile([P, 4 * D], BF16, name="dint_%d" % g, align_bytes=64)
            cols = slice(c * 128, (c + 1) * 128)
            new = dint[g][:, c * 512 : (c + 1) * 512].rearrange("p (n j) -> p n j", j=4)
            old = draw[g][:, :, cols].rearrange("p j n -> p n j")
            if c % 2 == 0:
                nc.scalar.copy(out=new, in_=old)
            else:
                nc.gpsimd.tensor_scalar(out=new, in0=old, scalar1=1.0, scalar2=0.0, op0=ALU.mult, op1=ALU.add)

        def dec_quantize(g, h):
            if h == 0:
                dcode[g] = keep.tile([P, D], U32, name="dcode_%d" % g, align_bytes=64)
                dscale[g] = keep.tile([P, D], U8, name="dscale_%d" % g, align_bytes=64)
            cols = slice(h * HALF, (h + 1) * HALF)
            nc.vector.quantize_mx(out=dcode[g][:, cols].bitcast(E4M3), scales=dscale[g][:, cols], in_=dint[g][:, h * 2048 : (h + 1) * 2048])


        mixed = [("f", 0), ("f", 1), ("f", 2), ("f", 3), ("n", 0), ("n", 1), ("f", 4), ("f", 5), ("n", 2)]
        steps = [(pair, kind, g) for pair in range(NPAIR) for kind, g in mixed]
        n_steps = len(steps)
        bank, mask, an, code, scale = {}, {}, {}, {}, {}

        split = {}

        def permute(s):
            pair, kind, g = steps[s]
            w, tile_words, off = x[kind, pair, g]
            t = work.tile([P, 2, 2, P], F32, name="split", bufs=5)
            nc.scalar.copy(
                out=t[:],
                in_=w.rearrange("p (a k) -> p a k", a=2)[:, :, off : off + 2 * P].rearrange("p a (w u) -> p a u w", u=2),
            )
            split[s] = t

        def transposes(s):
            pair, kind, g = steps[s]
            w, tile_words, off = x[kind, pair, g]
            b = psum_t.tile([P, 2, PAIR], F32, name="bank")
            for u in range(2):
                for a in range(2):
                    first = a * tile_words + off + u
                    some = split[s][:, a, u, :] if s in split else w[:, first : first + 2 * P - 1 : 2]
                    nc.tensor.transpose(b[:, u, a * P : (a + 1) * P], some, ident[:])
            bank[s] = b[:].rearrange("p u r -> p (u r)").bitcast(BF16).rearrange("p (u r e) -> p r u e", u=2, e=2)

        def scalar_mask(s):
            kind, g = steps[s][1:]
            m = work.tile([P, 4 * PAIR], BF16, name="mask_s", bufs=4)
            view = m[:].rearrange("p (u r e) -> p r u e", u=2, e=2)
            for u in range(2):
                for e in range(2):
                    j = 4 * g + 2 * u + e
                    nc.scalar.activation(
                        out=view[:, :, u, e],
                        in_=bank[s][:, :, u, e],
                        func=ACT.Sigmoid,
                        bias=shift[kind][:, j : j + 1],
                        scale=steep[kind][:, j : j + 1],
                    )
            mask[s] = view

        def make_mask(s):
            kind, g = steps[s][1:]
            m = work.tile([P, 4 * PAIR], BF16, name="mask")
            view = m[:].rearrange("p (r u e) -> p r u e", u=2, e=2)
            nc.vector.tensor_tensor(
                out=view,
                in0=bank[s],
                in1=th[kind][:, g : g + 1, :].rearrange("p o (u e) -> p o u e", u=2).to_broadcast([P, PAIR, 2, 2]),
                op=ALU.is_gt,
            )
            mask[s] = view

        def apply_mask(s):
            t = work.tile([P, 4 * PAIR], BF16, name="an", align_bytes=64)
            nc.vector.tensor_tensor(
                out=t[:].rearrange("p (r u e) -> p r u e", u=2, e=2),
                in0=bank[s],
                in1=mask[s],
                op=ALU.mult,
            )
            an[s] = t

        def quantize(s):
            c = keep.tile([P, PAIR], U32, name="code_%d" % s, align_bytes=64)
            sc = keep.tile([P, PAIR], U8, name="scale_%d" % s, align_bytes=64)
            nc.vector.quantize_mx(out=c[:].bitcast(E4M3), scales=sc[:], in_=an[s][:])
            code[s], scale[s] = c, sc

        acc = {}

        def multiply(group):
            for a in range(2):
                for h in range(2):
                    for s in group:
                        pair, kind, g = steps[s]
                        first = kind == "f" and g == 0
                        if first:
                            acc[pair, a, h] = psum_a.tile([P, HALF], F32, name="acc_%d%d" % (a, h))
                        if kind == "f":
                            rhs = words[g][:, h * 2 * HALF : (h + 1) * 2 * HALF].bitcast(E2M1)
                            rhs_scale = planes[:, g, h * HALF : (h + 1) * HALF]
                        else:
                            rhs = dcode[g][:, h * HALF : (h + 1) * HALF].bitcast(E4M3)
                            rhs_scale = dscale[g][:, h * HALF : (h + 1) * HALF]
                        nc.tensor.matmul_mx(
                            out=acc[pair, a, h][:],
                            lhsT=code[s][:, a * P : (a + 1) * P].bitcast(E4M3),
                            lhsT_scale=scale[s][:, a * P : (a + 1) * P],
                            rhs=rhs,
                            rhs_scale=rhs_scale,
                            start=first,
                            stop=(kind == "n" and g == NN - 1),
                        )

        def finish(pair):
            for a in range(2):
                row = pair * PAIR + a * P
                for h in range(2):
                    cols = slice(h * HALF, (h + 1) * HALF)
                    res = work.tile([P, HALF], F32, name="res", bufs=4)
                    nc.vector.tensor_tensor(out=res[:], in0=acc[pair, a, h][:], in1=bias_bc[:, cols], op=ALU.add)
                    nc.sync.dma_start(out=out[row : row + P, cols], in_=res[:])

        waves = [[0, 1], [2, 3], [4], [5], [6, 7], [8]] + [[s, s + 1] for s in range(9, n_steps, 2)]
        products = waves[:9] + [[15, 16], [17], [18, 19, 20], [21, 22], [23, 24], [25, 26]]
        dec_after = {2: 0, 3: 1, 5: 2}
        on_scalar = {w[-1] for w in waves if w[0] > 9 and len(w) == 2} | {9, 10}
        permuted = {s for s in range(13, n_steps)}

        prepare_sigmoid("f", NF)
        for g in range(NN):
            for c in range(8):
                dec_interleave(g, c)

        def prepare(w):
            if w < len(waves):
                for s in waves[w]:
                    transposes(s)
                    if s in on_scalar:
                        scalar_mask(s)

        prepare(0)
        for w in range(len(waves) + 1):
            if w + 2 < len(waves):
                for s in waves[w + 2]:
                    if s in permuted:
                        permute(s)
            if w > 3:
                prepare(w + 1)
            done = products[w - 1] if w > 0 else []
            multiply(done)
            if w <= 3:
                prepare(w + 1)
            now = waves[w] if w < len(waves) else []
            for s in now:
                if s not in on_scalar:
                    make_mask(s)
            for s in now:
                apply_mask(s)
            for s in now:
                quantize(s)
            if done and steps[done[-1]][1:] == mixed[-1]:
                finish(steps[done[-1]][0])
            if w in dec_after:
                dec_quantize(dec_after[w], 0)
                dec_quantize(dec_after[w], 1)
            if w == 0:
                prepare_sigmoid("n", NN)
